import numpy as np
import ml_dtypes


def mxq(x, axis, fmt="e4m3"):
    dtype, down = {"e4m3": (ml_dtypes.float8_e4m3fn, 7), "e5m2": (ml_dtypes.float8_e5m2, 14)}[fmt]
    v = np.moveaxis(np.asarray(x, np.float32).astype(ml_dtypes.bfloat16).astype(np.float64), axis, -1)
    blocks = v.reshape(v.shape[:-1] + (-1, 32))
    amax = np.abs(blocks).max(-1, keepdims=True)
    byte = np.maximum(np.where(amax > 0, np.frexp(amax)[1] - 1 + 127, 0) - down, 1)
    scale = np.exp2(byte - 127.0)
    codes = (blocks / scale).astype(np.float32).astype(dtype).astype(np.float64)
    return np.moveaxis((codes * scale).reshape(v.shape), -1, axis)


WIDE = False


def mx_kscale(k):
    if not WIDE:
        return np.ones(k)
    levels = np.array([10, -10, 5, -5, 0])
    if k % 512:
        return np.exp2(np.random.permutation(np.resize(levels, k // 32))).repeat(32)
    a = np.empty((k // 512, 16))
    for p in range(k // 512):
        a[p, :8] = np.random.permutation(np.resize(levels, 8))
        for g in range(8):
            far = levels[np.abs(levels - a[p, g]) >= 10]
            a[p, g + 8] = far[np.random.randint(len(far))]
    return np.exp2(a.ravel()).repeat(32)


def f64(x):
    return np.asarray(x).astype(np.float64)


def striped(idx):
    return np.tile(idx.reshape(-1, 16).T, (8, 1)).astype(np.uint16)


def unstriped(offs):
    return offs[:16].T.reshape(-1).astype(np.int64)


E2M1 = np.array([0.0, 0.5, 1.0, 1.5, 2.0, 3.0, 4.0, 6.0, -0.0, -0.5, -1.0, -1.5, -2.0, -3.0, -4.0, -6.0])


def pack_weight(w, fmt):
    k, n = w.shape
    w = f64(np.asarray(w, np.float32).astype(ml_dtypes.bfloat16)).reshape(k // 32, 32, n)
    amax = np.abs(w).max(1)
    if fmt == "e4m3":
        byte = np.frexp(amax)[1] - 1 + 127 - 7
    else:
        mant, ex = np.frexp(amax / 6.0)
        byte = np.where(mant > 0.5, ex, ex - 1) + 127
    byte = np.clip(np.where(amax > 0, byte, 1), 1, 254)
    scaled = (w * np.exp2(127.0 - byte)[:, None, :]).reshape(k, n).astype(np.float32)
    by_word = np.ascontiguousarray(scaled.reshape(k // 512, 128, 4, n).transpose(0, 1, 3, 2))
    if fmt == "e4m3":
        words = by_word.astype(ml_dtypes.float8_e4m3fn).view(np.uint8)
    else:
        c = by_word.astype(ml_dtypes.float4_e2m1fn).view(np.uint8) & 0xF
        words = (c[..., 0::2] | (c[..., 1::2] << 4)).reshape(k // 512, 128, 2 * n)
    return np.ascontiguousarray(words), np.ascontiguousarray(byte.astype(np.uint8).reshape(k // 512, 16, n))


def unpack_weight(words, scales, fmt):
    g, _, n = scales.shape
    words = np.ascontiguousarray(words).reshape(g, 128, n, -1)
    if fmt == "e4m3":
        vals = words.view(ml_dtypes.float8_e4m3fn).astype(np.float64)
    else:
        nib = np.empty((g, 128, n, 4), np.uint8)
        nib[..., 0::2] = words & 0xF
        nib[..., 1::2] = words >> 4
        vals = E2M1[nib]
    vals = vals * np.repeat(np.exp2(scales.astype(np.float64) - 127.0), 8, axis=1)[..., None]
    return vals.transpose(0, 1, 3, 2).reshape(g * 512, n)


def gelu(v):
    return 0.5 * v * (1.0 + np.tanh(np.sqrt(2.0 / np.pi) * (v + 0.044715 * v**3)))


def striped8(idx):
    return np.concatenate([v.reshape(-1, 16).T for v in idx]).astype(np.uint16)


def unstriped8(offs):
    return np.stack([offs[16 * g:16 * g + 16].T.reshape(-1) for g in range(8)]).astype(np.int64)


def runs(v, idx8):
    k = np.arange(v.shape[0])
    return v[k[:, None], idx8[k % 512 // 64]]


def put_heads(h, wgs, idx8, t2):
    r = np.arange(h.shape[0])
    page = np.zeros((h.shape[0], t2))
    page[r[:, None], idx8[r % 512 // 64]] = wgs[r // 4 % 128] * h
    return page


K, H, N, T, S, T2 = 512, 1024, 512, 2048, 1024, 2048

def setup_inputs():
    n = np.random.standard_normal
    s, u = mx_kscale(K)[:, None], mx_kscale(H)[:, None]
    tab_words, tab_scales = pack_weight(n((K, T)) * s, "e4m3")
    wb_words, wb_scales = pack_weight(n((K, H)) / np.sqrt(K) / s, "e2m1")
    wd_words, wd_scales = pack_weight(n((H, N)) / np.sqrt(H) / u, "e4m3")
    return {
        "tab_words": tab_words, "tab_scales": tab_scales,
        "wa": (n((K, H)) / np.sqrt(K) / s).astype(np.float32),
        "wb_words": wb_words, "wb_scales": wb_scales,
        "gain": (0.5 * np.exp(0.3 * n(H)) * u[:, 0]).astype(np.float32),
        "wc": (n((H, N)) / np.sqrt(H) / u).astype(np.float32),
        "wd_words": wd_words, "wd_scales": wd_scales,
        "wgo": np.repeat(np.random.uniform(0.5, 2.0, (8, S)), 16, axis=0).astype(np.float32),
        "offs": striped8(np.stack([np.random.permutation(T)[:S] for _ in range(8)])),
        "offs2": striped8(np.stack([np.random.permutation(T2)[:S] for _ in range(8)])),
    }

def reference(tab_words, tab_scales, wa, wb_words, wb_scales, gain, wc, wd_words, wd_scales, wgo, offs, offs2):
    v = runs(unpack_weight(tab_words, tab_scales, "e4m3"), unstriped8(offs))
    drive = mxq(f64(wa), 0, "e4m3").T @ v
    loss = unpack_weight(wb_words, wb_scales, "e2m1").T @ v
    h = f64(gain)[:, None] * (np.square(drive) - np.square(loss))
    hq = mxq(h, 0, "e4m3")
    force = mxq(f64(wc), 0, "e4m3").T @ hq
    speed = unpack_weight(wd_words, wd_scales, "e4m3").T @ hq
    y = force * speed
    return put_heads(y, f64(wgo), unstriped8(offs2), T2)

@@ -1,0 +1,257 @@
+from contextlib import ExitStack
+
+import concourse.mybir as mybir
+
+K, H, N, T, S, T2 = 512, 1024, 512, 2048, 1024, 2048
+FLOPS = 2 * 2 * K * H * S + 2 * 2 * H * N * S
+
+F32 = mybir.dt.float32
+BF16 = mybir.dt.bfloat16
+I32 = mybir.dt.int32
+U32 = mybir.dt.uint32
+U16 = mybir.dt.uint16
+U8 = mybir.dt.uint8
+FP8X4 = mybir.dt.float8_e4m3fn_x4
+FP4X4 = mybir.dt.float4_e2m1fn_x4
+ALU = mybir.AluOpType
+ACT = mybir.ActivationFunctionType
+
+P = 128
+PACK = 4
+PASS = P * PACK
+HP = H // PASS
+CHUNKS = (512, 512)
+PIECES = (512, 512)
+SHIFT = 14
+MOVED = 112
+YMODE = "g"
+CAST_V = ("wa0", "wa1", "wc0")
+PAGES = 3
+WC_AFTER = 3
+
+
+def tile_list_rowing_stroke_slots_kernel(
+    tc, tab_words, tab_scales, wa, wb_words, wb_scales, gain, wc, wd_words, wd_scales, wgo, offs, offs2, out
+):
+    nc = tc.nc
+    with ExitStack() as ctx:
+        keep = ctx.enter_context(tc.tile_pool(name="keep", bufs=1))
+        ring = ctx.enter_context(tc.tile_pool(name="ring", bufs=2))
+        psum = ctx.enter_context(tc.psum_pool(name="psum", bufs=8))
+
+        pick = keep.tile([P, S // 16], U16, name="pick")
+        nc.sync.dma_start(pick[:], offs)
+        place = keep.tile([P, S // 16], U16, name="place")
+        nc.sync.dma_start(place[:], offs2)
+        tabs = keep.tile([P, T], U8, name="tabs", tag="room_a", align_bytes=64)
+        ts32 = tab_scales[0].bitcast(I32)
+        for r in range(2):
+            nc.sync.dma_start(tabs[r:P:2, :].bitcast(I32), ts32[r:16:2, :].unsqueeze(1).to_broadcast([8, 8, T // 4]))
+        g = keep.tile([P, HP, PACK], F32, name="g")
+        nc.sync.dma_start(g[:], gain.rearrange("(a p t) -> p a t", a=HP, t=PACK))
+        tabw = keep.tile([P, T], I32, name="tabw", tag="room_t", align_bytes=64)
+        nc.sync.dma_start(tabw[:], tab_words[0].rearrange("p t i -> p (t i)").bitcast(I32))
+        wbw_raw = keep.tile([P, 2 * H], U8, name="wbw_raw", tag="room_c", align_bytes=64)
+        nc.sync.dma_start(wbw_raw[:].bitcast(I32), wb_words[0].bitcast(I32))
+        wbs_raw = keep.tile([P, H], U8, name="wbs_raw", tag="room_d", align_bytes=64)
+        for d in range(4):
+            nc.sync.dma_start(
+                wbs_raw[32 * d : 32 * d + 32, :].bitcast(I32),
+                wb_scales[0].bitcast(I32)[4 * d : 4 * d + 4, :].unsqueeze(0).to_broadcast([8, 4, H // 4]),
+            )
+
+        wa0_raw = []
+        for e in range(2):
+            raw = keep.tile([P, PACK, PASS // 2], F32, name="wa0_raw%d" % e, tag="room_e%d" % e, align_bytes=64)
+            nc.sync.dma_start(raw[:], wa[:, e * PASS // 2 : (e + 1) * PASS // 2].rearrange("(p j) c -> p j c", j=PACK))
+            wa0_raw.append(raw[:].rearrange("p j c -> p (j c)"))
+        vs = keep.tile([P, S], U8, name="vs", align_bytes=64)
+        nc.vector.memset(vs[:].bitcast(I32), 0)
+        half = keep.tile([P, HP * PACK], F32, name="half", tag="room_f")
+        nc.gpsimd.memset(half[:], 0.5)
+        pages = []
+        for i in range(2):
+            page = keep.tile([P, T2], F32, name="page%d" % i)
+            nc.vector.memset(page[:], 0.0)
+            pages.append(page)
+
+        picked = keep.tile([P, S], U8, name="picked", tag="room_b", align_bytes=64)
+        nc.vector.tensor_copy(picked[:], tabs[:].indirect(pick[:]))
+        nc.scalar.dma_start(vs[0:MOVED, :].bitcast(I32), picked[SHIFT : SHIFT + MOVED, :].bitcast(I32))
+        wa1_raw = keep.tile([P, PACK, PASS], F32, name="wa1_raw", tag="room_a", align_bytes=64)
+        nc.sync.dma_start(wa1_raw[:], wa[:, PASS : 2 * PASS].rearrange("(p j) c -> p j c", j=PACK))
+        wc0_raw = keep.tile([P, PACK * PASS], F32, name="wc0_raw", tag="room_b", align_bytes=64)
+        nc.sync.dma_start(wc0_raw[:], wc[0:PASS, :].rearrange("(p j) c -> p (j c)", j=PACK))
+
+        gabs = keep.tile([P, HP * PACK], F32, name="gabs")
+        gflat = g[:].rearrange("p a t -> p (a t)")
+        nc.scalar.activation(gabs[:], gflat, ACT.Abs)
+        sgn = keep.tile([P, HP * PACK], BF16, name="sgn")
+        nc.scalar.activation(sgn[:], gflat, ACT.Sign)
+        root = keep.tile([P, HP * PACK], F32, name="root")
+        nc.gpsimd.tensor_tensor(root[:], gabs[:], half[:], ALU.pow)
+        page = keep.tile([P, T2], F32, name="page2", tag="room_f")
+        nc.gpsimd.memset(page[:], 0.0)
+        pages.append(page)
+
+        starts = [sum(CHUNKS[:c]) for c in range(len(CHUNKS))]
+        piece_starts = [sum(PIECES[:c]) for c in range(len(PIECES))]
+        vw = []
+
+        def gather_words(c):
+            n, j0 = PIECES[c], piece_starts[c]
+            words = keep.tile([P, n], U32, name="vw%d" % c, align_bytes=64)
+            nc.vector.tensor_copy(words[:], tabw[:].bitcast(U32).indirect(pick[:, j0 // 16 : (j0 + n) // 16]))
+            vw.append(words)
+
+        gather_words(0)
+        wbw = keep.tile([P, 2 * H], U8, name="wbw", align_bytes=64)
+        nc.vector.tensor_copy(
+            wbw[:].bitcast(U16).rearrange("p (a t u m) -> p a u t m", a=HP, t=PACK, m=8),
+            wbw_raw[:].bitcast(U16).rearrange("p (a u m t) -> p a u t m", a=HP, t=PACK, m=8),
+        )
+        wbs = keep.tile([P, H], U8, name="wbs", align_bytes=64)
+        nc.vector.tensor_copy(
+            wbs[:].rearrange("p (a t u m) -> p a u t m", a=HP, t=PACK, m=16),
+            wbs_raw[:].rearrange("p (a u m t) -> p a u t m", a=HP, t=PACK, m=16),
+        )
+        wc1_raw = keep.tile([P, PACK * PASS], F32, name="wc1_raw", tag="room_c", align_bytes=64)
+        nc.sync.dma_start(wc1_raw[:], wc[PASS : 2 * PASS, :].rearrange("(p j) c -> p (j c)", j=PACK))
+        wds_raw = keep.tile([P, HP, N], U8, name="wds_raw", tag="room_d", align_bytes=64)
+        nc.vector.memset(wds_raw[:].bitcast(I32), 0)
+        for d in range(4):
+            nc.sync.dma_start(
+                wds_raw[32 * d : 32 * d + 4, :, :].bitcast(I32),
+                wd_scales.bitcast(I32)[:, 4 * d : 4 * d + 4, :].rearrange("a c w -> c a w"),
+            )
+
+        def quantise_weight(raw, name):
+            grouped = ring.tile([P, PACK * PASS], BF16, name="grouped", align_bytes=64)
+            width = P // len(raw)
+            for e in range(len(raw)):
+                dst = grouped[:].rearrange("p (t m j) -> p m t j", t=PACK, j=PACK)[:, e * width : (e + 1) * width]
+                src = raw[e].rearrange("p (j m t) -> p m t j", t=PACK, j=PACK)
+                if name in CAST_V:
+                    nc.vector.tensor_copy(dst, src)
+                else:
+                    nc.scalar.copy(dst, src)
+            codes = keep.tile([P, PASS], U32, name=name + "q", align_bytes=64)
+            scales = keep.tile([P, PASS], U8, name=name + "s", align_bytes=64)
+            nc.vector.quantize_mx(out=codes[:].bitcast(FP8X4), scales=scales[:], in_=grouped[:])
+            return codes, scales
+
+        waq = [None, None]
+        wcq = [None, None]
+        hq = {}
+
+        for c in range(len(CHUNKS)):
+            for a in range(HP):
+                codes = keep.tile([P, CHUNKS[c]], U32, name="hq%d_%d" % (c, a), align_bytes=64)
+                scales = keep.tile([P, CHUNKS[c]], U8, name="hs%d_%d" % (c, a), align_bytes=64)
+                hq[c, a] = (codes, scales)
+
+        def stage1(c, a):
+            n, j0 = PIECES[c], piece_starts[c]
+            sq = {}
+            for side in ("loss", "drive"):
+                sq[side] = ring.tile([P, PACK, n], F32, name="sq_" + side, bufs=3)
+                for t in range(PACK):
+                    bank = psum.tile([P, n], F32, name="bank")
+                    col = a * PASS + t * P
+                    if side == "loss":
+                        lhs, lhs_s = wbw[:, 2 * col : 2 * (col + P)].bitcast(FP4X4), wbs[:, col : col + P]
+                    else:
+                        lhs, lhs_s = waq[a][0][:, t * P : (t + 1) * P].bitcast(FP8X4), waq[a][1][:, t * P : (t + 1) * P]
+                    nc.tensor.matmul_mx(
+                        out=bank[:], lhsT=lhs, lhsT_scale=lhs_s, rhs=vw[c][:].bitcast(FP8X4),
+                        rhs_scale=vs[:, j0 : j0 + n], start=True, stop=True,
+                    )
+                    e = a * PACK + t
+                    nc.scalar.activation(sq[side][:, t, :], bank[:], ACT.Square, scale=root[:, e : e + 1])
+            diff = ring.tile([P, PACK * n], BF16, name="diff", align_bytes=64)
+            nc.vector.tensor_tensor(
+                diff[:].rearrange("p (u i t) -> p u t i", i=2, t=PACK),
+                sq["drive"][:].rearrange("p t (u i) -> p u t i", i=2),
+                sq["loss"][:].rearrange("p t (u i) -> p u t i", i=2),
+                ALU.subtract,
+            )
+            last = (c, a) == (len(PIECES) - 1, HP - 1)
+            signed = (keep if last else ring).tile([P, PACK * n], BF16, name="signed", align_bytes=64)
+            nc.vector.tensor_tensor(
+                signed[:].rearrange("p (j t) -> p j t", t=PACK),
+                diff[:].rearrange("p (j t) -> p j t", t=PACK),
+                sgn[:, a * PACK : (a + 1) * PACK].unsqueeze(1).to_broadcast([P, n, PACK]),
+                ALU.mult,
+            )
+            codes, scales = hq[j0 // PASS, a]
+            cols = slice(j0 % PASS, j0 % PASS + n)
+            nc.vector.quantize_mx(out=codes[:, cols].bitcast(FP8X4), scales=scales[:, cols], in_=signed[:])
+
+        def stage2(c, i):
+            n, j0 = CHUNKS[c], starts[c]
+            cols = slice(i * P, (i + 1) * P)
+            held = {}
+            for side in ("speed", "force"):
+                bank = psum.tile([P, n], F32, name="bank")
+                for a in range(HP):
+                    if side == "force":
+                        lhs, lhs_s = wcq[a][0][:, cols], wcq[a][1][:, cols]
+                    else:
+                        lhs, lhs_s = wdw[:, a, cols], wds[:, a, cols]
+                    nc.tensor.matmul_mx(
+                        out=bank[:], lhsT=lhs.bitcast(FP8X4), lhsT_scale=lhs_s,
+                        rhs=hq[c, a][0][:].bitcast(FP8X4), rhs_scale=hq[c, a][1][:],
+                        start=(a == 0), stop=(a == HP - 1),
+                    )
+                held[side] = ring.tile([P, n], F32, name="held_" + side, bufs=4)
+                nc.scalar.copy(held[side][:], bank[:])
+            window = pages[i % PAGES][:].indirect(place[:, j0 // 16 : (j0 + n) // 16])
+            weighted = ring.tile([P, n], F32, name="weighted", bufs=1)
+            if YMODE == "g":
+                if (c, i) == (0, 0):
+                    eng = nc.vector
+                    y = keep.tile([P, n], F32, name="y_first", tag="signed", align_bytes=64)
+                else:
+                    eng = nc.gpsimd
+                    y = ring.tile([P, n], F32, name="y", bufs=3)
+                eng.tensor_tensor(weighted[:], held["speed"][:], wg[:, j0 : j0 + n], ALU.mult)
+                eng.tensor_tensor(y[:], held["force"][:], weighted[:], ALU.mult)
+                nc.vector.tensor_copy(window, y[:])
+            else:
+                nc.vector.tensor_tensor(weighted[:], held["speed"][:], wg[:, j0 : j0 + n], ALU.mult)
+                nc.vector.tensor_tensor(window, held["force"][:], weighted[:], ALU.mult)
+
+        def second_weights():
+            wcq[0] = quantise_weight([wc0_raw[:]], "wc0")
+            wcq[1] = quantise_weight([wc1_raw[:]], "wc1")
+            nc.vector.tensor_copy(
+                wdw[:].rearrange("p a (i u m) -> p a u i m", i=PACK, m=4),
+                wdw_raw[:].bitcast(U32).rearrange("p a (u m i) -> p a u i m", i=PACK, m=4),
+            )
+            nc.vector.tensor_copy(
+                wds[:].rearrange("p a (i u m) -> p a u i m", i=PACK, m=16),
+                wds_raw[:].rearrange("p a (u m i) -> p a u i m", i=PACK, m=16),
+            )
+
+        wdw = keep.tile([P, HP, N], U32, name="wdw", align_bytes=64)
+        wds = keep.tile([P, HP, N], U8, name="wds", align_bytes=64)
+        waq[0] = quantise_weight(wa0_raw, "wa0")
+        wg = keep.tile([P, S], F32, name="wg", tag="room_e1", align_bytes=64)
+        nc.sync.dma_start(wg[:], wgo)
+        for c in range(1, len(PIECES)):
+            gather_words(c)
+        wdw_raw = keep.tile([P, HP, N], I32, name="wdw_raw", tag="room_t", align_bytes=64)
+        nc.sync.dma_start(wdw_raw[:], wd_words.rearrange("a p c i -> p a (c i)").bitcast(I32))
+        stage1(0, 0)
+        waq[1] = quantise_weight([wa1_raw[:].rearrange("p j c -> p (j c)")], "wa1")
+        units = [(c, a) for c in range(len(PIECES)) for a in range(HP)]
+        for u in range(1, len(units)):
+            stage1(*units[u])
+            if u == WC_AFTER:
+                second_weights()
+        for rows in (range(PAGES), range(PAGES, PACK)):
+            for c in range(len(CHUNKS)):
+                for i in rows:
+                    stage2(c, i)
+                    if c == len(CHUNKS) - 1:
+                        nc.sync.dma_start(out.rearrange("(p i) s -> p i s", i=PACK)[:, i, :], pages[i % PAGES][:])

@@ -19,15 +19,14 @@ ACT = mybir.ActivationFunctionType
 P = 128
 PACK = 4
 PASS = P * PACK
-HP = H // PASS
-CHUNKS = (512, 512)
+GROUP = 16
+H_PASSES = H // PASS
+CHUNK = 512
+CHUNKS = S // CHUNK
 PIECES = (512, 512)
-SHIFT = 14
-MOVED = 112
-YMODE = "g"
-CAST_V = ("wa0", "wa1", "wc0")
 PAGES = 3
-WC_AFTER = 3
+SHIFT = GROUP - 2
+MOVED = 112
 
 
 def tile_list_rowing_stroke_slots_kernel(
@@ -39,219 +38,219 @@ def tile_list_rowing_stroke_slots_kernel(
         ring = ctx.enter_context(tc.tile_pool(name="ring", bufs=2))
         psum = ctx.enter_context(tc.psum_pool(name="psum", bufs=8))
 
-        pick = keep.tile([P, S // 16], U16, name="pick")
-        nc.sync.dma_start(pick[:], offs)
-        place = keep.tile([P, S // 16], U16, name="place")
-        nc.sync.dma_start(place[:], offs2)
-        tabs = keep.tile([P, T], U8, name="tabs", tag="room_a", align_bytes=64)
-        ts32 = tab_scales[0].bitcast(I32)
-        for r in range(2):
-            nc.sync.dma_start(tabs[r:P:2, :].bitcast(I32), ts32[r:16:2, :].unsqueeze(1).to_broadcast([8, 8, T // 4]))
-        g = keep.tile([P, HP, PACK], F32, name="g")
-        nc.sync.dma_start(g[:], gain.rearrange("(a p t) -> p a t", a=HP, t=PACK))
-        tabw = keep.tile([P, T], I32, name="tabw", tag="room_t", align_bytes=64)
-        nc.sync.dma_start(tabw[:], tab_words[0].rearrange("p t i -> p (t i)").bitcast(I32))
-        wbw_raw = keep.tile([P, 2 * H], U8, name="wbw_raw", tag="room_c", align_bytes=64)
-        nc.sync.dma_start(wbw_raw[:].bitcast(I32), wb_words[0].bitcast(I32))
-        wbs_raw = keep.tile([P, H], U8, name="wbs_raw", tag="room_d", align_bytes=64)
-        for d in range(4):
-            nc.sync.dma_start(
-                wbs_raw[32 * d : 32 * d + 32, :].bitcast(I32),
-                wb_scales[0].bitcast(I32)[4 * d : 4 * d + 4, :].unsqueeze(0).to_broadcast([8, 4, H // 4]),
-            )
+        def entries(lists, j0, n):
+            return lists[:, j0 // GROUP : (j0 + n) // GROUP]
 
+        def rows_by_four(w):
+            return w.rearrange("(p j) c -> p j c", j=PACK)
+
+        pick = keep.tile([P, S // GROUP], U16, name="pick")
+        nc.sync.dma_start(pick[:], offs)
+        g = keep.tile([P, H_PASSES, PACK], F32, name="g")
+        nc.sync.dma_start(g[:], gain.rearrange("(a p t) -> p a t", a=H_PASSES, t=PACK))
+        tab_s = keep.tile([P, T], U8, name="tab_s", tag="room_wa1", align_bytes=64)
+        for r in range(2):
+            rows = tab_scales[0].bitcast(I32)[r::2, :]
+            nc.sync.dma_start(tab_s[r::2, :].bitcast(I32), rows.unsqueeze(1).to_broadcast([8, 8, T // 4]))
+        tab_w = keep.tile([P, T], I32, name="tab_w", tag="room_wd", align_bytes=64)
+        nc.sync.dma_start(tab_w[:], tab_words[0].rearrange("p t i -> p (t i)").bitcast(I32))
+        wb_w_raw = keep.tile([P, 2 * H], U8, name="wb_w_raw", tag="room_wc0", align_bytes=64)
+        nc.sync.dma_start(wb_w_raw[:].bitcast(I32), wb_words[0].bitcast(I32))
+        wb_s_raw = keep.tile([P, H], U8, name="wb_s_raw", tag="room_words", align_bytes=64)
+        for d in range(4):
+            rows = wb_scales[0].bitcast(I32)[4 * d : 4 * d + 4, :]
+            nc.sync.dma_start(
+                wb_s_raw[32 * d : 32 * d + 32, :].bitcast(I32), rows.unsqueeze(0).to_broadcast([8, 4, H // 4])
+            )
         wa0_raw = []
-        for e in range(2):
-            raw = keep.tile([P, PACK, PASS // 2], F32, name="wa0_raw%d" % e, tag="room_e%d" % e, align_bytes=64)
-            nc.sync.dma_start(raw[:], wa[:, e * PASS // 2 : (e + 1) * PASS // 2].rearrange("(p j) c -> p j c", j=PACK))
-            wa0_raw.append(raw[:].rearrange("p j c -> p (j c)"))
-        vs = keep.tile([P, S], U8, name="vs", align_bytes=64)
-        nc.vector.memset(vs[:].bitcast(I32), 0)
-        half = keep.tile([P, HP * PACK], F32, name="half", tag="room_f")
+        for e, room in enumerate(("wa0_low", "room_wgo")):
+            raw = keep.tile([P, PACK, PASS // 2], F32, name="wa0_raw%d" % e, tag=room, align_bytes=64)
+            nc.sync.dma_start(raw[:], rows_by_four(wa[:, e * PASS // 2 : (e + 1) * PASS // 2]))
+            wa0_raw.append(raw)
+        place = keep.tile([P, S // GROUP], U16, name="place")
+        nc.sync.dma_start(place[:], offs2)
+
+        v_s = []
+        for c in range(1):
+            plane = keep.tile([P, S // 1], U8, name="v_s%d" % c, align_bytes=64)
+            nc.gpsimd.memset(plane[:].bitcast(I32), 0)
+            v_s.append(plane)
+        half = keep.tile([P, H_PASSES * PACK], F32, name="half", tag="room_page", align_bytes=64)
         nc.gpsimd.memset(half[:], 0.5)
         pages = []
-        for i in range(2):
+        for i, engine in enumerate((nc.vector, nc.vector)):
             page = keep.tile([P, T2], F32, name="page%d" % i)
-            nc.vector.memset(page[:], 0.0)
+            engine.memset(page[:], 0.0)
             pages.append(page)
 
-        picked = keep.tile([P, S], U8, name="picked", tag="room_b", align_bytes=64)
-        nc.vector.tensor_copy(picked[:], tabs[:].indirect(pick[:]))
-        nc.scalar.dma_start(vs[0:MOVED, :].bitcast(I32), picked[SHIFT : SHIFT + MOVED, :].bitcast(I32))
-        wa1_raw = keep.tile([P, PACK, PASS], F32, name="wa1_raw", tag="room_a", align_bytes=64)
-        nc.sync.dma_start(wa1_raw[:], wa[:, PASS : 2 * PASS].rearrange("(p j) c -> p j c", j=PACK))
-        wc0_raw = keep.tile([P, PACK * PASS], F32, name="wc0_raw", tag="room_b", align_bytes=64)
-        nc.sync.dma_start(wc0_raw[:], wc[0:PASS, :].rearrange("(p j) c -> p (j c)", j=PACK))
+        for c, room in enumerate(("room_wc1",)):
+            picked = keep.tile([P, S // 1], U8, name="picked_s%d" % c, tag=room, align_bytes=64)
+            nc.vector.tensor_copy(picked[:], tab_s[:].indirect(entries(pick, c * S // 1, S // 1)))
+            nc.scalar.dma_start(v_s[c][0:MOVED, :].bitcast(I32), picked[SHIFT : SHIFT + MOVED, :].bitcast(I32))
+        wa1_raw = keep.tile([P, PACK, PASS], F32, name="wa1_raw", tag="room_wa1", align_bytes=64)
+        nc.sync.dma_start(wa1_raw[:], rows_by_four(wa[:, PASS : 2 * PASS]))
 
-        gabs = keep.tile([P, HP * PACK], F32, name="gabs")
-        gflat = g[:].rearrange("p a t -> p (a t)")
-        nc.scalar.activation(gabs[:], gflat, ACT.Abs)
-        sgn = keep.tile([P, HP * PACK], BF16, name="sgn")
-        nc.scalar.activation(sgn[:], gflat, ACT.Sign)
-        root = keep.tile([P, HP * PACK], F32, name="root")
-        nc.gpsimd.tensor_tensor(root[:], gabs[:], half[:], ALU.pow)
-        page = keep.tile([P, T2], F32, name="page2", tag="room_f")
+        g_flat = g[:].rearrange("p a t -> p (a t)")
+        g_abs = keep.tile([P, H_PASSES * PACK], F32, name="g_abs", tag="room_wd_s", align_bytes=64)
+        nc.scalar.activation(g_abs[:], g_flat, ACT.Abs)
+        g_sign = keep.tile([P, H_PASSES * PACK], BF16, name="g_sign")
+        nc.scalar.activation(g_sign[:], g_flat, ACT.Sign)
+        g_root = keep.tile([P, H_PASSES * PACK], F32, name="g_root")
+        nc.gpsimd.tensor_tensor(g_root[:], g_abs[:], half[:], ALU.pow)
+
+        wd_s_raw = keep.tile([P, H_PASSES, N], U8, name="wd_s_raw", tag="room_wd_s", align_bytes=64)
+        nc.gpsimd.memset(wd_s_raw[:].bitcast(I32), 0)
+        for d in range(4):
+            rows = wd_scales.bitcast(I32)[:, 4 * d : 4 * d + 4, :]
+            nc.sync.dma_start(wd_s_raw[32 * d : 32 * d + 4, :, :].bitcast(I32), rows.rearrange("a c w -> c a w"))
+
+        page = keep.tile([P, T2], F32, name="page2", tag="room_page", align_bytes=64)
         nc.gpsimd.memset(page[:], 0.0)
         pages.append(page)
 
-        starts = [sum(CHUNKS[:c]) for c in range(len(CHUNKS))]
-        piece_starts = [sum(PIECES[:c]) for c in range(len(PIECES))]
-        vw = []
-
-        def gather_words(c):
-            n, j0 = PIECES[c], piece_starts[c]
-            words = keep.tile([P, n], U32, name="vw%d" % c, align_bytes=64)
-            nc.vector.tensor_copy(words[:], tabw[:].bitcast(U32).indirect(pick[:, j0 // 16 : (j0 + n) // 16]))
-            vw.append(words)
-
-        gather_words(0)
-        wbw = keep.tile([P, 2 * H], U8, name="wbw", align_bytes=64)
-        nc.vector.tensor_copy(
-            wbw[:].bitcast(U16).rearrange("p (a t u m) -> p a u t m", a=HP, t=PACK, m=8),
-            wbw_raw[:].bitcast(U16).rearrange("p (a u m t) -> p a u t m", a=HP, t=PACK, m=8),
-        )
-        wbs = keep.tile([P, H], U8, name="wbs", align_bytes=64)
-        nc.vector.tensor_copy(
-            wbs[:].rearrange("p (a t u m) -> p a u t m", a=HP, t=PACK, m=16),
-            wbs_raw[:].rearrange("p (a u m t) -> p a u t m", a=HP, t=PACK, m=16),
-        )
-        wc1_raw = keep.tile([P, PACK * PASS], F32, name="wc1_raw", tag="room_c", align_bytes=64)
-        nc.sync.dma_start(wc1_raw[:], wc[PASS : 2 * PASS, :].rearrange("(p j) c -> p (j c)", j=PACK))
-        wds_raw = keep.tile([P, HP, N], U8, name="wds_raw", tag="room_d", align_bytes=64)
-        nc.vector.memset(wds_raw[:].bitcast(I32), 0)
-        for d in range(4):
-            nc.sync.dma_start(
-                wds_raw[32 * d : 32 * d + 4, :, :].bitcast(I32),
-                wd_scales.bitcast(I32)[:, 4 * d : 4 * d + 4, :].rearrange("a c w -> c a w"),
+        def reorder_columns(engine, dst, src, run):
+            engine.tensor_copy(
+                dst.rearrange("p (a t u m) -> p a u t m", a=H_PASSES, t=PACK, m=run),
+                src.rearrange("p (a u m t) -> p a u t m", a=H_PASSES, t=PACK, m=run),
             )
 
-        def quantise_weight(raw, name):
+        starts = [sum(PIECES[:c]) for c in range(len(PIECES))]
+        v_w = []
+
+        def gather_words(c, room):
+            words = keep.tile([P, PIECES[c]], U32, name="v_w%d" % c, tag=room, align_bytes=64)
+            nc.vector.tensor_copy(words[:], tab_w[:].bitcast(U32).indirect(entries(pick, starts[c], PIECES[c])))
+            v_w.append(words)
+
+        def quantise_weight(name, parts):
             grouped = ring.tile([P, PACK * PASS], BF16, name="grouped", align_bytes=64)
-            width = P // len(raw)
-            for e in range(len(raw)):
-                dst = grouped[:].rearrange("p (t m j) -> p m t j", t=PACK, j=PACK)[:, e * width : (e + 1) * width]
-                src = raw[e].rearrange("p (j m t) -> p m t j", t=PACK, j=PACK)
-                if name in CAST_V:
-                    nc.vector.tensor_copy(dst, src)
-                else:
-                    nc.scalar.copy(dst, src)
-            codes = keep.tile([P, PASS], U32, name=name + "q", align_bytes=64)
-            scales = keep.tile([P, PASS], U8, name=name + "s", align_bytes=64)
+            width = P // len(parts)
+            for e, (engine, raw) in enumerate(parts):
+                dst = grouped[:].rearrange("p (x y m j) -> p x m j y", x=2, y=2, j=PACK)
+                engine(dst[:, :, e * width : (e + 1) * width], raw.rearrange("p j (m x y) -> p x m j y", x=2, y=2))
+            codes = keep.tile([P, PASS], U32, name=name + "_w", align_bytes=64)
+            scales = keep.tile([P, PASS], U8, name=name + "_s", align_bytes=64)
             nc.vector.quantize_mx(out=codes[:].bitcast(FP8X4), scales=scales[:], in_=grouped[:])
             return codes, scales
 
-        waq = [None, None]
-        wcq = [None, None]
-        hq = {}
+        gather_words(0, "v_w0")
+        wb_w = keep.tile([P, 2 * H], U8, name="wb_w", align_bytes=64)
+        reorder_columns(nc.vector, wb_w[:].bitcast(U16), wb_w_raw[:].bitcast(U16), 8)
+        wb_s = keep.tile([P, H], U8, name="wb_s", align_bytes=64)
+        reorder_columns(nc.vector, wb_s[:], wb_s_raw[:], 16)
+        wc_raw = []
+        for a in range(H_PASSES):
+            raw = keep.tile([P, PACK, N], F32, name="wc_raw%d" % a, tag="room_wc%d" % a, align_bytes=64)
+            nc.sync.dma_start(raw[:], rows_by_four(wc[a * PASS : (a + 1) * PASS, :]))
+            wc_raw.append(raw)
+        wa_q = [quantise_weight("wa0", [(nc.scalar.copy, wa0_raw[0][:]), (nc.vector.tensor_copy, wa0_raw[1][:])])]
+        wg = keep.tile([P, S], F32, name="wg", tag="room_wgo", align_bytes=64)
+        nc.sync.dma_start(wg[:], wgo)
+        for c in range(1, len(PIECES)):
+            gather_words(c, "v_w%d" % c)
+        wd_w_raw = keep.tile([P, H_PASSES * N], I32, name="wd_w_raw", tag="room_wd", align_bytes=64)
+        nc.sync.dma_start(
+            wd_w_raw[:].rearrange("p (a c) -> p a c", a=H_PASSES), wd_words.rearrange("a p c i -> p a (c i)").bitcast(I32)
+        )
 
-        for c in range(len(CHUNKS)):
-            for a in range(HP):
-                codes = keep.tile([P, CHUNKS[c]], U32, name="hq%d_%d" % (c, a), align_bytes=64)
-                scales = keep.tile([P, CHUNKS[c]], U8, name="hs%d_%d" % (c, a), align_bytes=64)
-                hq[c, a] = (codes, scales)
+        h_q = {}
+        for c in range(CHUNKS):
+            for a in range(H_PASSES):
+                codes = keep.tile([P, CHUNK], U32, name="h_w%d_%d" % (c, a), align_bytes=64)
+                scales = keep.tile([P, CHUNK], U8, name="h_s%d_%d" % (c, a), align_bytes=64)
+                h_q[c, a] = (codes, scales)
 
-        def stage1(c, a):
-            n, j0 = PIECES[c], piece_starts[c]
-            sq = {}
+        def first_stage(c, a):
+            n, j0 = PIECES[c], starts[c]
+            plane = v_s[j0 // (S // 1)][:, j0 % (S // 1) : j0 % (S // 1) + n]
+            squares = {}
             for side in ("loss", "drive"):
-                sq[side] = ring.tile([P, PACK, n], F32, name="sq_" + side, bufs=3)
+                squares[side] = ring.tile([P, PACK, n], F32, name="sq_" + side, bufs=3)
                 for t in range(PACK):
-                    bank = psum.tile([P, n], F32, name="bank")
-                    col = a * PASS + t * P
                     if side == "loss":
-                        lhs, lhs_s = wbw[:, 2 * col : 2 * (col + P)].bitcast(FP4X4), wbs[:, col : col + P]
+                        col = a * PASS + t * P
+                        lhs, lhs_s = wb_w[:, 2 * col : 2 * (col + P)].bitcast(FP4X4), wb_s[:, col : col + P]
                     else:
-                        lhs, lhs_s = waq[a][0][:, t * P : (t + 1) * P].bitcast(FP8X4), waq[a][1][:, t * P : (t + 1) * P]
+                        cols = slice(t * P, (t + 1) * P)
+                        lhs, lhs_s = wa_q[a][0][:, cols].bitcast(FP8X4), wa_q[a][1][:, cols]
+                    bank = psum.tile([P, n], F32, name="bank")
                     nc.tensor.matmul_mx(
-                        out=bank[:], lhsT=lhs, lhsT_scale=lhs_s, rhs=vw[c][:].bitcast(FP8X4),
-                        rhs_scale=vs[:, j0 : j0 + n], start=True, stop=True,
+                        out=bank[:], lhsT=lhs, lhsT_scale=lhs_s, rhs=v_w[c][:].bitcast(FP8X4), rhs_scale=plane,
+                        start=True, stop=True,
                     )
                     e = a * PACK + t
-                    nc.scalar.activation(sq[side][:, t, :], bank[:], ACT.Square, scale=root[:, e : e + 1])
+                    nc.scalar.activation(squares[side][:, t, :], bank[:], ACT.Square, scale=g_root[:, e : e + 1])
             diff = ring.tile([P, PACK * n], BF16, name="diff", align_bytes=64)
             nc.vector.tensor_tensor(
                 diff[:].rearrange("p (u i t) -> p u t i", i=2, t=PACK),
-                sq["drive"][:].rearrange("p t (u i) -> p u t i", i=2),
-                sq["loss"][:].rearrange("p t (u i) -> p u t i", i=2),
+                squares["drive"][:].rearrange("p t (u i) -> p u t i", i=2),
+                squares["loss"][:].rearrange("p t (u i) -> p u t i", i=2),
                 ALU.subtract,
             )
-            last = (c, a) == (len(PIECES) - 1, HP - 1)
-            signed = (keep if last else ring).tile([P, PACK * n], BF16, name="signed", align_bytes=64)
+            last = (c, a) == (len(PIECES) - 1, H_PASSES - 1)
+            if last:
+                signed = keep.tile([P, PACK * n], BF16, name="signed_last", tag="room_y", align_bytes=64)
+            else:
+                signed = ring.tile([P, PACK * n], BF16, name="signed", align_bytes=64)
             nc.vector.tensor_tensor(
                 signed[:].rearrange("p (j t) -> p j t", t=PACK),
                 diff[:].rearrange("p (j t) -> p j t", t=PACK),
-                sgn[:, a * PACK : (a + 1) * PACK].unsqueeze(1).to_broadcast([P, n, PACK]),
+                g_sign[:, a * PACK : (a + 1) * PACK].unsqueeze(1).to_broadcast([P, n, PACK]),
                 ALU.mult,
             )
-            codes, scales = hq[j0 // PASS, a]
-            cols = slice(j0 % PASS, j0 % PASS + n)
+            codes, scales = h_q[j0 // CHUNK, a]
+            cols = slice(j0 % CHUNK, j0 % CHUNK + n)
             nc.vector.quantize_mx(out=codes[:, cols].bitcast(FP8X4), scales=scales[:, cols], in_=signed[:])
 
-        def stage2(c, i):
-            n, j0 = CHUNKS[c], starts[c]
+        def second_stage(c, i):
+            j0 = c * CHUNK
             cols = slice(i * P, (i + 1) * P)
             held = {}
             for side in ("speed", "force"):
-                bank = psum.tile([P, n], F32, name="bank")
-                for a in range(HP):
+                bank = psum.tile([P, CHUNK], F32, name="bank")
+                for a in range(H_PASSES):
                     if side == "force":
-                        lhs, lhs_s = wcq[a][0][:, cols], wcq[a][1][:, cols]
+                        lhs, lhs_s = wc_q[a][0][:, cols], wc_q[a][1][:, cols]
                     else:
-                        lhs, lhs_s = wdw[:, a, cols], wds[:, a, cols]
+                        wd_cols = slice(a * N + i * P, a * N + (i + 1) * P)
+                        lhs, lhs_s = wd_w[:, wd_cols], wd_s[:, wd_cols]
                     nc.tensor.matmul_mx(
                         out=bank[:], lhsT=lhs.bitcast(FP8X4), lhsT_scale=lhs_s,
-                        rhs=hq[c, a][0][:].bitcast(FP8X4), rhs_scale=hq[c, a][1][:],
-                        start=(a == 0), stop=(a == HP - 1),
+                        rhs=h_q[c, a][0][:].bitcast(FP8X4), rhs_scale=h_q[c, a][1][:],
+                        start=(a == 0), stop=(a == H_PASSES - 1),
                     )
-                held[side] = ring.tile([P, n], F32, name="held_" + side, bufs=4)
+                held[side] = ring.tile([P, CHUNK], F32, name="held_" + side, bufs=4)
                 nc.scalar.copy(held[side][:], bank[:])
-            window = pages[i % PAGES][:].indirect(place[:, j0 // 16 : (j0 + n) // 16])
-            weighted = ring.tile([P, n], F32, name="weighted", bufs=1)
-            if YMODE == "g":
-                if (c, i) == (0, 0):
-                    eng = nc.vector
-                    y = keep.tile([P, n], F32, name="y_first", tag="signed", align_bytes=64)
-                else:
-                    eng = nc.gpsimd
-                    y = ring.tile([P, n], F32, name="y", bufs=3)
-                eng.tensor_tensor(weighted[:], held["speed"][:], wg[:, j0 : j0 + n], ALU.mult)
-                eng.tensor_tensor(y[:], held["force"][:], weighted[:], ALU.mult)
-                nc.vector.tensor_copy(window, y[:])
+            weighted = ring.tile([P, CHUNK], F32, name="weighted", bufs=1)
+            if (c, i) == (0, 0):
+                engine = nc.vector
+                y = keep.tile([P, CHUNK], F32, name="y_first", tag="room_y", align_bytes=64)
             else:
-                nc.vector.tensor_tensor(weighted[:], held["speed"][:], wg[:, j0 : j0 + n], ALU.mult)
-                nc.vector.tensor_tensor(window, held["force"][:], weighted[:], ALU.mult)
+                engine = nc.gpsimd
+                y = ring.tile([P, CHUNK], F32, name="y", bufs=3)
+            engine.tensor_tensor(weighted[:], held["speed"][:], wg[:, j0 : j0 + CHUNK], ALU.mult)
+            engine.tensor_tensor(y[:], held["force"][:], weighted[:], ALU.mult)
+            nc.vector.tensor_copy(pages[i % PAGES][:].indirect(entries(place, j0, CHUNK)), y[:])
 
-        def second_weights():
-            wcq[0] = quantise_weight([wc0_raw[:]], "wc0")
-            wcq[1] = quantise_weight([wc1_raw[:]], "wc1")
-            nc.vector.tensor_copy(
-                wdw[:].rearrange("p a (i u m) -> p a u i m", i=PACK, m=4),
-                wdw_raw[:].bitcast(U32).rearrange("p a (u m i) -> p a u i m", i=PACK, m=4),
-            )
-            nc.vector.tensor_copy(
-                wds[:].rearrange("p a (i u m) -> p a u i m", i=PACK, m=16),
-                wds_raw[:].rearrange("p a (u m i) -> p a u i m", i=PACK, m=16),
-            )
-
-        wdw = keep.tile([P, HP, N], U32, name="wdw", align_bytes=64)
-        wds = keep.tile([P, HP, N], U8, name="wds", align_bytes=64)
-        waq[0] = quantise_weight(wa0_raw, "wa0")
-        wg = keep.tile([P, S], F32, name="wg", tag="room_e1", align_bytes=64)
-        nc.sync.dma_start(wg[:], wgo)
-        for c in range(1, len(PIECES)):
-            gather_words(c)
-        wdw_raw = keep.tile([P, HP, N], I32, name="wdw_raw", tag="room_t", align_bytes=64)
-        nc.sync.dma_start(wdw_raw[:], wd_words.rearrange("a p c i -> p a (c i)").bitcast(I32))
-        stage1(0, 0)
-        waq[1] = quantise_weight([wa1_raw[:].rearrange("p j c -> p (j c)")], "wa1")
-        units = [(c, a) for c in range(len(PIECES)) for a in range(HP)]
+        first_stage(0, 0)
+        wa_q.append(quantise_weight("wa1", [(nc.vector.tensor_copy, wa1_raw[:])]))
+        wd_s = keep.tile([P, H_PASSES * N], U8, name="wd_s", align_bytes=64)
+        reorder_columns(nc.vector, wd_s[:], wd_s_raw[:].rearrange("p a c -> p (a c)"), 16)
+        wd_w = keep.tile([P, H_PASSES * N], U32, name="wd_w", align_bytes=64)
+        nc.vector.tensor_copy(
+            wd_w[:].rearrange("p (a x y m) -> p a x m y", a=H_PASSES, x=2, y=2),
+            wd_w_raw[:].bitcast(U32).rearrange("p (a m x y) -> p a x m y", a=H_PASSES, x=2, y=2),
+        )
+        wc_q = [quantise_weight("wc0", [(nc.vector.tensor_copy, wc_raw[0][:])])]
+        units = [(c, a) for c in range(len(PIECES)) for a in range(H_PASSES)]
         for u in range(1, len(units)):
-            stage1(*units[u])
-            if u == WC_AFTER:
-                second_weights()
-        for rows in (range(PAGES), range(PAGES, PACK)):
-            for c in range(len(CHUNKS)):
-                for i in rows:
-                    stage2(c, i)
-                    if c == len(CHUNKS) - 1:
+            first_stage(*units[u])
+            if u == 1:
+                wc_q.append(quantise_weight("wc1", [(nc.vector.tensor_copy, wc_raw[1][:])]))
+
+        for slots in (range(PAGES), range(PAGES, PACK)):
+            for c in range(CHUNKS):
+                for i in slots:
+                    second_stage(c, i)
+                    if c == CHUNKS - 1:
                         nc.sync.dma_start(out.rearrange("(p i) s -> p i s", i=PACK)[:, i, :], pages[i % PAGES][:])

@@ -23,7 +23,9 @@ GROUP = 16
 H_PASSES = H // PASS
 CHUNK = 512
 CHUNKS = S // CHUNK
-PIECES = (512, 512)
+PIECES = (512,)
+EARLY = 0
+LOSS, DRIVE = 0, 1
 PAGES = 3
 SHIFT = GROUP - 2
 MOVED = 112
@@ -48,13 +50,13 @@ def tile_list_rowing_stroke_slots_kernel(
         nc.sync.dma_start(pick[:], offs)
         g = keep.tile([P, H_PASSES, PACK], F32, name="g")
         nc.sync.dma_start(g[:], gain.rearrange("(a p t) -> p a t", a=H_PASSES, t=PACK))
-        tab_s = keep.tile([P, T], U8, name="tab_s", tag="room_wa1", align_bytes=64)
+        tab_s = keep.tile([P, T], U8, name="tab_s", tag="room_late", align_bytes=64)
         for r in range(2):
             rows = tab_scales[0].bitcast(I32)[r::2, :]
             nc.sync.dma_start(tab_s[r::2, :].bitcast(I32), rows.unsqueeze(1).to_broadcast([8, 8, T // 4]))
         tab_w = keep.tile([P, T], I32, name="tab_w", tag="room_wd", align_bytes=64)
         nc.sync.dma_start(tab_w[:], tab_words[0].rearrange("p t i -> p (t i)").bitcast(I32))
-        wb_w_raw = keep.tile([P, 2 * H], U8, name="wb_w_raw", tag="room_wc0", align_bytes=64)
+        wb_w_raw = keep.tile([P, 2 * H], U8, name="wb_w_raw", align_bytes=64)
         nc.sync.dma_start(wb_w_raw[:].bitcast(I32), wb_words[0].bitcast(I32))
         wb_s_raw = keep.tile([P, H], U8, name="wb_s_raw", tag="room_words", align_bytes=64)
         for d in range(4):
@@ -63,7 +65,7 @@ def tile_list_rowing_stroke_slots_kernel(
                 wb_s_raw[32 * d : 32 * d + 32, :].bitcast(I32), rows.unsqueeze(0).to_broadcast([8, 4, H // 4])
             )
         wa0_raw = []
-        for e, room in enumerate(("wa0_low", "room_wgo")):
+        for e, room in enumerate(("wa0_low", "wa0_high")):
             raw = keep.tile([P, PACK, PASS // 2], F32, name="wa0_raw%d" % e, tag=room, align_bytes=64)
             nc.sync.dma_start(raw[:], rows_by_four(wa[:, e * PASS // 2 : (e + 1) * PASS // 2]))
             wa0_raw.append(raw)
@@ -78,17 +80,24 @@ def tile_list_rowing_stroke_slots_kernel(
         half = keep.tile([P, H_PASSES * PACK], F32, name="half", tag="room_page", align_bytes=64)
         nc.gpsimd.memset(half[:], 0.5)
         pages = []
-        for i, engine in enumerate((nc.vector, nc.vector)):
+        for i, engine in enumerate((nc.vector, nc.gpsimd)):
             page = keep.tile([P, T2], F32, name="page%d" % i)
             engine.memset(page[:], 0.0)
             pages.append(page)
 
-        for c, room in enumerate(("room_wc1",)):
+        for c, room in enumerate(("picked",)):
             picked = keep.tile([P, S // 1], U8, name="picked_s%d" % c, tag=room, align_bytes=64)
             nc.vector.tensor_copy(picked[:], tab_s[:].indirect(entries(pick, c * S // 1, S // 1)))
-            nc.scalar.dma_start(v_s[c][0:MOVED, :].bitcast(I32), picked[SHIFT : SHIFT + MOVED, :].bitcast(I32))
-        wa1_raw = keep.tile([P, PACK, PASS], F32, name="wa1_raw", tag="room_wa1", align_bytes=64)
-        nc.sync.dma_start(wa1_raw[:], rows_by_four(wa[:, PASS : 2 * PASS]))
+            nc.sync.dma_start(v_s[c][0:MOVED, :].bitcast(I32), picked[SHIFT : SHIFT + MOVED, :].bitcast(I32))
+        late = keep.tile([P, 3 * PACK * PASS + S], F32, name="late", tag="room_late", align_bytes=64)
+        big = PACK * PASS
+        wa1_raw = late[:, 0:big].rearrange("p (j c) -> p j c", j=PACK)
+        wc_raw = [late[:, (1 + a) * big : (2 + a) * big].rearrange("p (j c) -> p j c", j=PACK) for a in range(H_PASSES)]
+        wg = late[:, 3 * big :]
+        nc.sync.dma_start(wa1_raw, rows_by_four(wa[:, PASS : 2 * PASS]))
+        nc.sync.dma_start(wc_raw[0], rows_by_four(wc[0:PASS, :]))
+        nc.sync.dma_start(wc_raw[1], rows_by_four(wc[PASS : 2 * PASS, :]))
+        nc.sync.dma_start(wg, wgo)
 
         g_flat = g[:].rearrange("p a t -> p (a t)")
         g_abs = keep.tile([P, H_PASSES * PACK], F32, name="g_abs", tag="room_wd_s", align_bytes=64)
@@ -118,8 +127,8 @@ def tile_list_rowing_stroke_slots_kernel(
         v_w = []
 
         def gather_words(c, room):
-            words = keep.tile([P, PIECES[c]], U32, name="v_w%d" % c, tag=room, align_bytes=64)
-            nc.vector.tensor_copy(words[:], tab_w[:].bitcast(U32).indirect(entries(pick, starts[c], PIECES[c])))
+            words = keep.tile([P, CHUNK], U32, name="v_w%d" % c, tag=room, align_bytes=64)
+            nc.vector.tensor_copy(words[:], tab_w[:].bitcast(U32).indirect(entries(pick, c * CHUNK, CHUNK)))
             v_w.append(words)
 
         def quantise_weight(name, parts):
@@ -138,15 +147,8 @@ def tile_list_rowing_stroke_slots_kernel(
         reorder_columns(nc.vector, wb_w[:].bitcast(U16), wb_w_raw[:].bitcast(U16), 8)
         wb_s = keep.tile([P, H], U8, name="wb_s", align_bytes=64)
         reorder_columns(nc.vector, wb_s[:], wb_s_raw[:], 16)
-        wc_raw = []
-        for a in range(H_PASSES):
-            raw = keep.tile([P, PACK, N], F32, name="wc_raw%d" % a, tag="room_wc%d" % a, align_bytes=64)
-            nc.sync.dma_start(raw[:], rows_by_four(wc[a * PASS : (a + 1) * PASS, :]))
-            wc_raw.append(raw)
         wa_q = [quantise_weight("wa0", [(nc.scalar.copy, wa0_raw[0][:]), (nc.vector.tensor_copy, wa0_raw[1][:])])]
-        wg = keep.tile([P, S], F32, name="wg", tag="room_wgo", align_bytes=64)
-        nc.sync.dma_start(wg[:], wgo)
-        for c in range(1, len(PIECES)):
+        for c in range(1, CHUNKS):
             gather_words(c, "v_w%d" % c)
         wd_w_raw = keep.tile([P, H_PASSES * N], I32, name="wd_w_raw", tag="room_wd", align_bytes=64)
         nc.sync.dma_start(
@@ -160,34 +162,37 @@ def tile_list_rowing_stroke_slots_kernel(
                 scales = keep.tile([P, CHUNK], U8, name="h_s%d_%d" % (c, a), align_bytes=64)
                 h_q[c, a] = (codes, scales)
 
-        def first_stage(c, a):
-            n, j0 = PIECES[c], starts[c]
+        def first_stage(j0, n, a, per_bank):
             plane = v_s[j0 // (S // 1)][:, j0 % (S // 1) : j0 % (S // 1) + n]
-            squares = {}
-            for side in ("loss", "drive"):
-                squares[side] = ring.tile([P, PACK, n], F32, name="sq_" + side, bufs=3)
+            words = v_w[j0 // CHUNK][:, j0 % CHUNK : j0 % CHUNK + n].bitcast(FP8X4)
+            squares = ring.tile([P, PACK, 2, n], F32, name="squares", bufs=3)
+
+            def reading(dst, side, t):
+                if side == LOSS:
+                    col = a * PASS + t * P
+                    lhs, lhs_s = wb_w[:, 2 * col : 2 * (col + P)].bitcast(FP4X4), wb_s[:, col : col + P]
+                else:
+                    cols = slice(t * P, (t + 1) * P)
+                    lhs, lhs_s = wa_q[a][0][:, cols].bitcast(FP8X4), wa_q[a][1][:, cols]
+                nc.tensor.matmul_mx(
+                    out=dst, lhsT=lhs, lhsT_scale=lhs_s, rhs=words, rhs_scale=plane, start=True, stop=True
+                )
+
+            for first in range(0, 2, per_bank):
                 for t in range(PACK):
-                    if side == "loss":
-                        col = a * PASS + t * P
-                        lhs, lhs_s = wb_w[:, 2 * col : 2 * (col + P)].bitcast(FP4X4), wb_s[:, col : col + P]
-                    else:
-                        cols = slice(t * P, (t + 1) * P)
-                        lhs, lhs_s = wa_q[a][0][:, cols].bitcast(FP8X4), wa_q[a][1][:, cols]
-                    bank = psum.tile([P, n], F32, name="bank")
-                    nc.tensor.matmul_mx(
-                        out=bank[:], lhsT=lhs, lhsT_scale=lhs_s, rhs=v_w[c][:].bitcast(FP8X4), rhs_scale=plane,
-                        start=True, stop=True,
-                    )
-                    e = a * PACK + t
-                    nc.scalar.activation(squares[side][:, t, :], bank[:], ACT.Square, scale=g_root[:, e : e + 1])
+                    bank = psum.tile([P, per_bank, n], F32, name="bank")
+                    for e in range(per_bank):
+                        reading(bank[:, e, :], first + e, t)
+                    scale = g_root[:, a * PACK + t : a * PACK + t + 1]
+                    nc.scalar.activation(squares[:, t, first : first + per_bank, :], bank[:], ACT.Square, scale=scale)
             diff = ring.tile([P, PACK * n], BF16, name="diff", align_bytes=64)
             nc.vector.tensor_tensor(
                 diff[:].rearrange("p (u i t) -> p u t i", i=2, t=PACK),
-                squares["drive"][:].rearrange("p t (u i) -> p u t i", i=2),
-                squares["loss"][:].rearrange("p t (u i) -> p u t i", i=2),
+                squares[:, :, DRIVE, :].rearrange("p t (u i) -> p u t i", i=2),
+                squares[:, :, LOSS, :].rearrange("p t (u i) -> p u t i", i=2),
                 ALU.subtract,
             )
-            last = (c, a) == (len(PIECES) - 1, H_PASSES - 1)
+            last = (j0 + n, a) == (S, H_PASSES - 1)
             if last:
                 signed = keep.tile([P, PACK * n], BF16, name="signed_last", tag="room_y", align_bytes=64)
             else:
@@ -222,7 +227,12 @@ def tile_list_rowing_stroke_slots_kernel(
                 held[side] = ring.tile([P, CHUNK], F32, name="held_" + side, bufs=4)
                 nc.scalar.copy(held[side][:], bank[:])
             weighted = ring.tile([P, CHUNK], F32, name="weighted", bufs=1)
-            if (c, i) == (0, 0):
+            window = pages[i % PAGES][:].indirect(entries(place, j0, CHUNK))
+            if c == 0 and i < EARLY:
+                nc.vector.tensor_tensor(weighted[:], held["speed"][:], wg[:, j0 : j0 + CHUNK], ALU.mult)
+                nc.vector.tensor_tensor(window, held["force"][:], weighted[:], ALU.mult)
+                return
+            if (c, i) == (0, EARLY):
                 engine = nc.vector
                 y = keep.tile([P, CHUNK], F32, name="y_first", tag="room_y", align_bytes=64)
             else:
@@ -230,10 +240,12 @@ def tile_list_rowing_stroke_slots_kernel(
                 y = ring.tile([P, CHUNK], F32, name="y", bufs=3)
             engine.tensor_tensor(weighted[:], held["speed"][:], wg[:, j0 : j0 + CHUNK], ALU.mult)
             engine.tensor_tensor(y[:], held["force"][:], weighted[:], ALU.mult)
-            nc.vector.tensor_copy(pages[i % PAGES][:].indirect(entries(place, j0, CHUNK)), y[:])
+            nc.vector.tensor_copy(window, y[:])
 
-        first_stage(0, 0)
-        wa_q.append(quantise_weight("wa1", [(nc.vector.tensor_copy, wa1_raw[:])]))
+        units = [(0,256,0,1),(256,256,0,2),(0,512,1,1),(512,512,0,1),(512,256,1,2),(768,256,1,2)]
+        first_stage(*units[0])
+        first_stage(*units[1])
+        wa_q.append(quantise_weight("wa1", [(nc.vector.tensor_copy, wa1_raw)]))
         wd_s = keep.tile([P, H_PASSES * N], U8, name="wd_s", align_bytes=64)
         reorder_columns(nc.vector, wd_s[:], wd_s_raw[:].rearrange("p a c -> p (a c)"), 16)
         wd_w = keep.tile([P, H_PASSES * N], U32, name="wd_w", align_bytes=64)
@@ -241,16 +253,19 @@ def tile_list_rowing_stroke_slots_kernel(
             wd_w[:].rearrange("p (a x y m) -> p a x m y", a=H_PASSES, x=2, y=2),
             wd_w_raw[:].bitcast(U32).rearrange("p (a m x y) -> p a x m y", a=H_PASSES, x=2, y=2),
         )
-        wc_q = [quantise_weight("wc0", [(nc.vector.tensor_copy, wc_raw[0][:])])]
-        units = [(c, a) for c in range(len(PIECES)) for a in range(H_PASSES)]
-        for u in range(1, len(units)):
+        wc_q = [quantise_weight("wc0", [(nc.vector.tensor_copy, wc_raw[0])])]
+        for u in range(2, len(units)):
+            if u == 2:
+                for i in range(EARLY):
+                    second_stage(0, i)
             first_stage(*units[u])
-            if u == 1:
-                wc_q.append(quantise_weight("wc1", [(nc.vector.tensor_copy, wc_raw[1][:])]))
+            if u == 2:
+                wc_q.append(quantise_weight("wc1", [(nc.vector.tensor_copy, wc_raw[1])]))
 
         for slots in (range(PAGES), range(PAGES, PACK)):
             for c in range(CHUNKS):
                 for i in slots:
-                    second_stage(c, i)
+                    if c > 0 or i >= EARLY:
+                        second_stage(c, i)
                     if c == CHUNKS - 1:
                         nc.sync.dma_start(out.rearrange("(p i) s -> p i s", i=PACK)[:, i, :], pages[i % PAGES][:])

from contextlib import ExitStack

import concourse.mybir as mybir

K, H, N, T, S, T2 = 512, 1024, 512, 2048, 1024, 2048
FLOPS = 2 * 2 * K * H * S + 2 * 2 * H * N * S

F32 = mybir.dt.float32
BF16 = mybir.dt.bfloat16
I32 = mybir.dt.int32
U32 = mybir.dt.uint32
U16 = mybir.dt.uint16
U8 = mybir.dt.uint8
FP8X4 = mybir.dt.float8_e4m3fn_x4
FP4X4 = mybir.dt.float4_e2m1fn_x4
ALU = mybir.AluOpType
ACT = mybir.ActivationFunctionType

P = 128
PACK = 4
PASS = P * PACK
GROUP = 16
H_PASSES = H // PASS
CHUNK = 512
CHUNKS = S // CHUNK
PIECES = (512,)
EARLY = 0
LOSS, DRIVE = 0, 1
PAGES = 3
SHIFT = GROUP - 2
MOVED = 112


def tile_list_rowing_stroke_slots_kernel(
    tc, tab_words, tab_scales, wa, wb_words, wb_scales, gain, wc, wd_words, wd_scales, wgo, offs, offs2, out
):
    nc = tc.nc
    with ExitStack() as ctx:
        keep = ctx.enter_context(tc.tile_pool(name="keep", bufs=1))
        ring = ctx.enter_context(tc.tile_pool(name="ring", bufs=2))
        psum = ctx.enter_context(tc.psum_pool(name="psum", bufs=8))

        def entries(lists, j0, n):
            return lists[:, j0 // GROUP : (j0 + n) // GROUP]

        def rows_by_four(w):
            return w.rearrange("(p j) c -> p j c", j=PACK)

        pick = keep.tile([P, S // GROUP], U16, name="pick")
        nc.sync.dma_start(pick[:], offs)
        g = keep.tile([P, H_PASSES, PACK], F32, name="g")
        nc.sync.dma_start(g[:], gain.rearrange("(a p t) -> p a t", a=H_PASSES, t=PACK))
        tab_s = keep.tile([P, T], U8, name="tab_s", tag="room_late", align_bytes=64)
        for r in range(2):
            rows = tab_scales[0].bitcast(I32)[r::2, :]
            nc.sync.dma_start(tab_s[r::2, :].bitcast(I32), rows.unsqueeze(1).to_broadcast([8, 8, T // 4]))
        tab_w = keep.tile([P, T], I32, name="tab_w", tag="room_wd", align_bytes=64)
        nc.sync.dma_start(tab_w[:], tab_words[0].rearrange("p t i -> p (t i)").bitcast(I32))
        wb_w_raw = keep.tile([P, 2 * H], U8, name="wb_w_raw", align_bytes=64)
        nc.sync.dma_start(wb_w_raw[:].bitcast(I32), wb_words[0].bitcast(I32))
        wb_s_raw = keep.tile([P, H], U8, name="wb_s_raw", tag="room_words", align_bytes=64)
        for d in range(4):
            rows = wb_scales[0].bitcast(I32)[4 * d : 4 * d + 4, :]
            nc.sync.dma_start(
                wb_s_raw[32 * d : 32 * d + 32, :].bitcast(I32), rows.unsqueeze(0).to_broadcast([8, 4, H // 4])
            )
        wa0_raw = []
        for e, room in enumerate(("wa0_low", "wa0_high")):
            raw = keep.tile([P, PACK, PASS // 2], F32, name="wa0_raw%d" % e, tag=room, align_bytes=64)
            nc.sync.dma_start(raw[:], rows_by_four(wa[:, e * PASS // 2 : (e + 1) * PASS // 2]))
            wa0_raw.append(raw)
        place = keep.tile([P, S // GROUP], U16, name="place")
        nc.sync.dma_start(place[:], offs2)

        v_s = []
        for c in range(1):
            plane = keep.tile([P, S // 1], U8, name="v_s%d" % c, align_bytes=64)
            nc.gpsimd.memset(plane[:].bitcast(I32), 0)
            v_s.append(plane)
        half = keep.tile([P, H_PASSES * PACK], F32, name="half", tag="room_page", align_bytes=64)
        nc.gpsimd.memset(half[:], 0.5)
        pages = []
        for i, engine in enumerate((nc.vector, nc.gpsimd)):
            page = keep.tile([P, T2], F32, name="page%d" % i)
            engine.memset(page[:], 0.0)
            pages.append(page)

        for c, room in enumerate(("picked",)):
            picked = keep.tile([P, S // 1], U8, name="picked_s%d" % c, tag=room, align_bytes=64)
            nc.vector.tensor_copy(picked[:], tab_s[:].indirect(entries(pick, c * S // 1, S // 1)))
            nc.sync.dma_start(v_s[c][0:MOVED, :].bitcast(I32), picked[SHIFT : SHIFT + MOVED, :].bitcast(I32))
        late = keep.tile([P, 3 * PACK * PASS + S], F32, name="late", tag="room_late", align_bytes=64)
        big = PACK * PASS
        wa1_raw = late[:, 0:big].rearrange("p (j c) -> p j c", j=PACK)
        wc_raw = [late[:, (1 + a) * big : (2 + a) * big].rearrange("p (j c) -> p j c", j=PACK) for a in range(H_PASSES)]
        wg = late[:, 3 * big :]
        nc.sync.dma_start(wa1_raw, rows_by_four(wa[:, PASS : 2 * PASS]))
        nc.sync.dma_start(wc_raw[0], rows_by_four(wc[0:PASS, :]))
        nc.sync.dma_start(wc_raw[1], rows_by_four(wc[PASS : 2 * PASS, :]))
        nc.sync.dma_start(wg, wgo)

        g_flat = g[:].rearrange("p a t -> p (a t)")
        g_abs = keep.tile([P, H_PASSES * PACK], F32, name="g_abs", tag="room_wd_s", align_bytes=64)
        nc.scalar.activation(g_abs[:], g_flat, ACT.Abs)
        g_sign = keep.tile([P, H_PASSES * PACK], BF16, name="g_sign")
        nc.scalar.activation(g_sign[:], g_flat, ACT.Sign)
        g_root = keep.tile([P, H_PASSES * PACK], F32, name="g_root")
        nc.gpsimd.tensor_tensor(g_root[:], g_abs[:], half[:], ALU.pow)

        wd_s_raw = keep.tile([P, H_PASSES, N], U8, name="wd_s_raw", tag="room_wd_s", align_bytes=64)
        nc.gpsimd.memset(wd_s_raw[:].bitcast(I32), 0)
        for d in range(4):
            rows = wd_scales.bitcast(I32)[:, 4 * d : 4 * d + 4, :]
            nc.sync.dma_start(wd_s_raw[32 * d : 32 * d + 4, :, :].bitcast(I32), rows.rearrange("a c w -> c a w"))

        page = keep.tile([P, T2], F32, name="page2", tag="room_page", align_bytes=64)
        nc.gpsimd.memset(page[:], 0.0)
        pages.append(page)

        def reorder_columns(engine, dst, src, run):
            engine.tensor_copy(
                dst.rearrange("p (a t u m) -> p a u t m", a=H_PASSES, t=PACK, m=run),
                src.rearrange("p (a u m t) -> p a u t m", a=H_PASSES, t=PACK, m=run),
            )

        starts = [sum(PIECES[:c]) for c in range(len(PIECES))]
        v_w = []

        def gather_words(c, room):
            words = keep.tile([P, CHUNK], U32, name="v_w%d" % c, tag=room, align_bytes=64)
            nc.vector.tensor_copy(words[:], tab_w[:].bitcast(U32).indirect(entries(pick, c * CHUNK, CHUNK)))
            v_w.append(words)

        def quantise_weight(name, parts):
            grouped = ring.tile([P, PACK * PASS], BF16, name="grouped", align_bytes=64)
            width = P // len(parts)
            for e, (engine, raw) in enumerate(parts):
                dst = grouped[:].rearrange("p (x y m j) -> p x m j y", x=2, y=2, j=PACK)
                engine(dst[:, :, e * width : (e + 1) * width], raw.rearrange("p j (m x y) -> p x m j y", x=2, y=2))
            codes = keep.tile([P, PASS], U32, name=name + "_w", align_bytes=64)
            scales = keep.tile([P, PASS], U8, name=name + "_s", align_bytes=64)
            nc.vector.quantize_mx(out=codes[:].bitcast(FP8X4), scales=scales[:], in_=grouped[:])
            return codes, scales

        gather_words(0, "v_w0")
        wb_w = keep.tile([P, 2 * H], U8, name="wb_w", align_bytes=64)
        reorder_columns(nc.vector, wb_w[:].bitcast(U16), wb_w_raw[:].bitcast(U16), 8)
        wb_s = keep.tile([P, H], U8, name="wb_s", align_bytes=64)
        reorder_columns(nc.vector, wb_s[:], wb_s_raw[:], 16)
        wa_q = [quantise_weight("wa0", [(nc.scalar.copy, wa0_raw[0][:]), (nc.vector.tensor_copy, wa0_raw[1][:])])]
        for c in range(1, CHUNKS):
            gather_words(c, "v_w%d" % c)
        wd_w_raw = keep.tile([P, H_PASSES * N], I32, name="wd_w_raw", tag="room_wd", align_bytes=64)
        nc.sync.dma_start(
            wd_w_raw[:].rearrange("p (a c) -> p a c", a=H_PASSES), wd_words.rearrange("a p c i -> p a (c i)").bitcast(I32)
        )

        h_q = {}
        for c in range(CHUNKS):
            for a in range(H_PASSES):
                codes = keep.tile([P, CHUNK], U32, name="h_w%d_%d" % (c, a), align_bytes=64)
                scales = keep.tile([P, CHUNK], U8, name="h_s%d_%d" % (c, a), align_bytes=64)
                h_q[c, a] = (codes, scales)

        def first_stage(j0, n, a, per_bank):
            plane = v_s[j0 // (S // 1)][:, j0 % (S // 1) : j0 % (S // 1) + n]
            words = v_w[j0 // CHUNK][:, j0 % CHUNK : j0 % CHUNK + n].bitcast(FP8X4)
            squares = ring.tile([P, PACK, 2, n], F32, name="squares", bufs=3)

            def reading(dst, side, t):
                if side == LOSS:
                    col = a * PASS + t * P
                    lhs, lhs_s = wb_w[:, 2 * col : 2 * (col + P)].bitcast(FP4X4), wb_s[:, col : col + P]
                else:
                    cols = slice(t * P, (t + 1) * P)
                    lhs, lhs_s = wa_q[a][0][:, cols].bitcast(FP8X4), wa_q[a][1][:, cols]
                nc.tensor.matmul_mx(
                    out=dst, lhsT=lhs, lhsT_scale=lhs_s, rhs=words, rhs_scale=plane, start=True, stop=True
                )

            for first in range(0, 2, per_bank):
                for t in range(PACK):
                    bank = psum.tile([P, per_bank, n], F32, name="bank")
                    for e in range(per_bank):
                        reading(bank[:, e, :], first + e, t)
                    scale = g_root[:, a * PACK + t : a * PACK + t + 1]
                    nc.scalar.activation(squares[:, t, first : first + per_bank, :], bank[:], ACT.Square, scale=scale)
            diff = ring.tile([P, PACK * n], BF16, name="diff", align_bytes=64)
            nc.vector.tensor_tensor(
                diff[:].rearrange("p (u i t) -> p u t i", i=2, t=PACK),
                squares[:, :, DRIVE, :].rearrange("p t (u i) -> p u t i", i=2),
                squares[:, :, LOSS, :].rearrange("p t (u i) -> p u t i", i=2),
                ALU.subtract,
            )
            last = (j0 + n, a) == (S, H_PASSES - 1)
            if last:
                signed = keep.tile([P, PACK * n], BF16, name="signed_last", tag="room_y", align_bytes=64)
            else:
                signed = ring.tile([P, PACK * n], BF16, name="signed", align_bytes=64)
            nc.vector.tensor_tensor(
                signed[:].rearrange("p (j t) -> p j t", t=PACK),
                diff[:].rearrange("p (j t) -> p j t", t=PACK),
                g_sign[:, a * PACK : (a + 1) * PACK].unsqueeze(1).to_broadcast([P, n, PACK]),
                ALU.mult,
            )
            codes, scales = h_q[j0 // CHUNK, a]
            cols = slice(j0 % CHUNK, j0 % CHUNK + n)
            nc.vector.quantize_mx(out=codes[:, cols].bitcast(FP8X4), scales=scales[:, cols], in_=signed[:])

        def second_stage(c, i):
            j0 = c * CHUNK
            cols = slice(i * P, (i + 1) * P)
            held = {}
            for side in ("speed", "force"):
                bank = psum.tile([P, CHUNK], F32, name="bank")
                for a in range(H_PASSES):
                    if side == "force":
                        lhs, lhs_s = wc_q[a][0][:, cols], wc_q[a][1][:, cols]
                    else:
                        wd_cols = slice(a * N + i * P, a * N + (i + 1) * P)
                        lhs, lhs_s = wd_w[:, wd_cols], wd_s[:, wd_cols]
                    nc.tensor.matmul_mx(
                        out=bank[:], lhsT=lhs.bitcast(FP8X4), lhsT_scale=lhs_s,
                        rhs=h_q[c, a][0][:].bitcast(FP8X4), rhs_scale=h_q[c, a][1][:],
                        start=(a == 0), stop=(a == H_PASSES - 1),
                    )
                held[side] = ring.tile([P, CHUNK], F32, name="held_" + side, bufs=4)
                nc.scalar.copy(held[side][:], bank[:])
            weighted = ring.tile([P, CHUNK], F32, name="weighted", bufs=1)
            window = pages[i % PAGES][:].indirect(entries(place, j0, CHUNK))
            if c == 0 and i < EARLY:
                nc.vector.tensor_tensor(weighted[:], held["speed"][:], wg[:, j0 : j0 + CHUNK], ALU.mult)
                nc.vector.tensor_tensor(window, held["force"][:], weighted[:], ALU.mult)
                return
            if (c, i) == (0, EARLY):
                engine = nc.vector
                y = keep.tile([P, CHUNK], F32, name="y_first", tag="room_y", align_bytes=64)
            else:
                engine = nc.gpsimd
                y = ring.tile([P, CHUNK], F32, name="y", bufs=3)
            engine.tensor_tensor(weighted[:], held["speed"][:], wg[:, j0 : j0 + CHUNK], ALU.mult)
            engine.tensor_tensor(y[:], held["force"][:], weighted[:], ALU.mult)
            nc.vector.tensor_copy(window, y[:])

        units = [(0,256,0,1),(256,256,0,2),(0,512,1,1),(512,512,0,1),(512,256,1,2),(768,256,1,2)]
        first_stage(*units[0])
        first_stage(*units[1])
        wa_q.append(quantise_weight("wa1", [(nc.vector.tensor_copy, wa1_raw)]))
        wd_s = keep.tile([P, H_PASSES * N], U8, name="wd_s", align_bytes=64)
        reorder_columns(nc.vector, wd_s[:], wd_s_raw[:].rearrange("p a c -> p (a c)"), 16)
        wd_w = keep.tile([P, H_PASSES * N], U32, name="wd_w", align_bytes=64)
        nc.vector.tensor_copy(
            wd_w[:].rearrange("p (a x y m) -> p a x m y", a=H_PASSES, x=2, y=2),
            wd_w_raw[:].bitcast(U32).rearrange("p (a m x y) -> p a x m y", a=H_PASSES, x=2, y=2),
        )
        wc_q = [quantise_weight("wc0", [(nc.vector.tensor_copy, wc_raw[0])])]
        for u in range(2, len(units)):
            if u == 2:
                for i in range(EARLY):
                    second_stage(0, i)
            first_stage(*units[u])
            if u == 2:
                wc_q.append(quantise_weight("wc1", [(nc.vector.tensor_copy, wc_raw[1])]))

        for slots in (range(PAGES), range(PAGES, PACK)):
            for c in range(CHUNKS):
                for i in slots:
                    if c > 0 or i >= EARLY:
                        second_stage(c, i)
                    if c == CHUNKS - 1:
                        nc.sync.dma_start(out.rearrange("(p i) s -> p i s", i=PACK)[:, i, :], pages[i % PAGES][:])
